import numpy as np
import ml_dtypes


def mxq(x, axis, fmt="e4m3"):
    dtype, down = {"e4m3": (ml_dtypes.float8_e4m3fn, 7), "e5m2": (ml_dtypes.float8_e5m2, 14)}[fmt]
    v = np.moveaxis(np.asarray(x, np.float32).astype(ml_dtypes.bfloat16).astype(np.float64), axis, -1)
    blocks = v.reshape(v.shape[:-1] + (-1, 32))
    amax = np.abs(blocks).max(-1, keepdims=True)
    byte = np.maximum(np.where(amax > 0, np.frexp(amax)[1] - 1 + 127, 0) - down, 1)
    scale = np.exp2(byte - 127.0)
    codes = (blocks / scale).astype(np.float32).astype(dtype).astype(np.float64)
    return np.moveaxis((codes * scale).reshape(v.shape), -1, axis)


WIDE = False


def mx_kscale(k):
    if not WIDE:
        return np.ones(k)
    levels = np.array([10, -10, 5, -5, 0])
    if k % 512:
        return np.exp2(np.random.permutation(np.resize(levels, k // 32))).repeat(32)
    a = np.empty((k // 512, 16))
    for p in range(k // 512):
        a[p, :8] = np.random.permutation(np.resize(levels, 8))
        for g in range(8):
            far = levels[np.abs(levels - a[p, g]) >= 10]
            a[p, g + 8] = far[np.random.randint(len(far))]
    return np.exp2(a.ravel()).repeat(32)


def f64(x):
    return np.asarray(x).astype(np.float64)


def striped(idx):
    return np.tile(idx.reshape(-1, 16).T, (8, 1)).astype(np.uint16)


def unstriped(offs):
    return offs[:16].T.reshape(-1).astype(np.int64)


E2M1 = np.array([0.0, 0.5, 1.0, 1.5, 2.0, 3.0, 4.0, 6.0, -0.0, -0.5, -1.0, -1.5, -2.0, -3.0, -4.0, -6.0])


def pack_weight(w, fmt):
    k, n = w.shape
    w = f64(np.asarray(w, np.float32).astype(ml_dtypes.bfloat16)).reshape(k // 32, 32, n)
    amax = np.abs(w).max(1)
    if fmt == "e4m3":
        byte = np.frexp(amax)[1] - 1 + 127 - 7
    else:
        mant, ex = np.frexp(amax / 6.0)
        byte = np.where(mant > 0.5, ex, ex - 1) + 127
    byte = np.clip(np.where(amax > 0, byte, 1), 1, 254)
    scaled = (w * np.exp2(127.0 - byte)[:, None, :]).reshape(k, n).astype(np.float32)
    by_word = np.ascontiguousarray(scaled.reshape(k // 512, 128, 4, n).transpose(0, 1, 3, 2))
    if fmt == "e4m3":
        words = by_word.astype(ml_dtypes.float8_e4m3fn).view(np.uint8)
    else:
        c = by_word.astype(ml_dtypes.float4_e2m1fn).view(np.uint8) & 0xF
        words = (c[..., 0::2] | (c[..., 1::2] << 4)).reshape(k // 512, 128, 2 * n)
    return np.ascontiguousarray(words), np.ascontiguousarray(byte.astype(np.uint8).reshape(k // 512, 16, n))


def unpack_weight(words, scales, fmt):
    g, _, n = scales.shape
    words = np.ascontiguousarray(words).reshape(g, 128, n, -1)
    if fmt == "e4m3":
        vals = words.view(ml_dtypes.float8_e4m3fn).astype(np.float64)
    else:
        nib = np.empty((g, 128, n, 4), np.uint8)
        nib[..., 0::2] = words & 0xF
        nib[..., 1::2] = words >> 4
        vals = E2M1[nib]
    vals = vals * np.repeat(np.exp2(scales.astype(np.float64) - 127.0), 8, axis=1)[..., None]
    return vals.transpose(0, 1, 3, 2).reshape(g * 512, n)


def gelu(v):
    return 0.5 * v * (1.0 + np.tanh(np.sqrt(2.0 / np.pi) * (v + 0.044715 * v**3)))


def bf(x):
    return np.asarray(x, np.float32).astype(ml_dtypes.bfloat16)


def planes(Y):
    n, m = Y.shape
    b = f64(bf(Y)).reshape(n // 32, 32, m)
    amax = np.abs(b).max(1)
    byte = np.clip(np.where(amax > 0, np.frexp(amax)[1] - 1 + 127 - 7, 1), 1, 254)
    codes = (b * np.exp2(127.0 - byte)[:, None, :]).reshape(n, m).astype(np.float32).astype(ml_dtypes.float8_e4m3fn).view(np.uint8)
    words = codes.reshape(n // 512, 128, 4, m).transpose(0, 1, 3, 2)
    return np.ascontiguousarray(words), np.ascontiguousarray(byte.astype(np.uint8).reshape(n // 512, 16, m))


K, T, S, H, T2, P, N = 1024, 4096, 1024, 512, 2048, 512, 512

def setup_inputs():
    n = np.random.standard_normal
    s = mx_kscale(K)[:, None]
    u = mx_kscale(H)[:, None]
    d = {}
    d["tab_words"], d["tab_scales"] = pack_weight(n((K, T)) * s, "e4m3")
    d["offs"] = striped(np.random.permutation(T)[:S])
    d["offs2"] = striped(np.random.permutation(T2)[:S])
    d["offs3"] = striped(np.random.permutation(T2)[:P])
    d["w1"] = (n((K, H)) / K**0.5 / s * u.T).astype(np.float32)
    d["w2_words"], d["w2_scales"] = pack_weight(n((K, H)) / K**0.5 / s * u.T, "e2m1")
    d["w3"] = (n((K, H)) / K**0.5 / s * u.T).astype(np.float32)
    d["wgs"] = np.exp(0.3 * n((128, S))).astype(np.float32)
    d["page0"] = (n((H, T2)) * u).astype(np.float32)
    d["bias"] = (0.7 * n(H) * u[:, 0]).astype(np.float32)
    d["w4_words"], d["w4_scales"] = pack_weight(n((H, N)) / H**0.5 / u, "e2m1")
    d["w5"] = (n((H, N)) / H**0.5 / u).astype(np.float32)
    d["flav"] = n((N, P)).astype(np.float32)
    return d

def reference(tab_words, tab_scales, offs, offs2, offs3, w1, w2_words, w2_scales, w3, wgs, page0, bias, w4_words, w4_scales, w5, flav):
    v = unpack_weight(tab_words, tab_scales, "e4m3")[:, unstriped(offs)]
    w2 = unpack_weight(w2_words, w2_scales, "e2m1")
    w4 = unpack_weight(w4_words, w4_scales, "e2m1")
    a = mxq(f64(w1), 0, "e4m3").T @ v
    b = w2.T @ v
    e = mxq(f64(w3), 0, "e4m3").T @ v
    h = np.maximum(a, b) + np.minimum(a, e)
    page = f64(page0).copy()
    page[:, unstriped(offs2)] = np.tile(f64(wgs), (H // 128, 1)) * h
    x = page[:, unstriped(offs3)] + f64(bias)[:, None]
    xq = mxq(x, 0, "e4m3")
    m1 = w4.T @ xq
    m2 = mxq(f64(w5), 0, "e4m3").T @ xq
    y = f64(flav) * m1 + m2
    words, scales = planes(page)
    return y, page, words, scales

@@ -1,0 +1,286 @@
+from contextlib import ExitStack
+
+import concourse.mybir as mybir
+from concourse.masks import make_identity
+
+K, T, S, H, T2, PICK, N = 1024, 4096, 1024, 512, 2048, 512, 512
+FLOPS = 2 * (3 * K * H * S + 2 * H * N * PICK)
+
+F32 = mybir.dt.float32
+BF16 = mybir.dt.bfloat16
+I32 = mybir.dt.int32
+U32 = mybir.dt.uint32
+U16 = mybir.dt.uint16
+U8 = mybir.dt.uint8
+FP8X4 = mybir.dt.float8_e4m3fn_x4
+FP4X4 = mybir.dt.float4_e2m1fn_x4
+ALU = mybir.AluOpType
+ACT = mybir.ActivationFunctionType
+
+P = 128
+PACK = 4
+K_PASS = P * PACK
+PASSES = K // K_PASS
+BANK = 512
+J_TILES = S // P
+QUADS = 4
+QUAD = 32
+CHUNKS = T2 // BANK
+LIST_COLS = 16
+
+
+def tile_list_freezer_texture_page_kernel(
+    tc, tab_words, tab_scales, offs, offs2, offs3, w1, w2_words, w2_scales, w3, wgs, page0, bias,
+    w4_words, w4_scales, w5, flav, out_0, out_1, out_2, out_3,
+):
+    nc = tc.nc
+    with ExitStack() as ctx:
+        lists = ctx.enter_context(tc.tile_pool(name="lists", bufs=1))
+        keep = ctx.enter_context(tc.tile_pool(name="keep", bufs=1))
+        psum = ctx.enter_context(tc.psum_pool(name="psum", bufs=1))
+
+        def sb(shape, dtype, name, tag=None):
+            return keep.tile(shape, dtype, name=name, tag=tag or name, align_bytes=64)
+
+        def bank(index, name):
+            return psum.tile([P, BANK], F32, name=name, tag="bank%d" % index)
+
+        def dealt(bank_tile):
+            return bank_tile[:].rearrange("p (m t) -> p t m", t=PACK)
+
+        def load_rows(w_rows, name, tag):
+            raw = sb([P, PACK, H], F32, name, tag)
+            nc.sync.dma_start(out=raw[:], in_=w_rows.rearrange("(p i) c -> p i c", i=PACK))
+            return raw
+
+        def load_scale_rows(plane, scales):
+            for q in range(QUADS):
+                nc.sync.dma_start(
+                    out=plane[QUAD * q : QUAD * q + 4, :, :].bitcast(I32),
+                    in_=scales[:, 4 * q : 4 * q + 4, :].rearrange("a r c -> r a c").bitcast(I32),
+                )
+
+        def weave(copy, raw, name, tag):
+            woven = sb([P, H, PACK], BF16, name, tag)
+            copy(
+                out=woven[:].rearrange("p (c u) i -> p c i u", u=4),
+                in_=raw[:].rearrange("p i (c u) -> p c i u", u=4),
+            )
+            return woven
+
+        def quantize(woven, name, tag=None):
+            width = woven.shape[1]
+            codes = sb([P, width], U32, name + "_codes", tag)
+            scales = sb([P, width], U8, name + "_scales")
+            nc.vector.quantize_mx(
+                out=codes[:].bitcast(FP8X4), scales=scales[:], in_=woven[:].rearrange("p c i -> p (c i)")
+            )
+            return codes, scales
+
+        tab_rows = sb([P, T], U8, "tab_rows")
+        v_scales = sb([P, PASSES, S], U8, "v_scales")
+        w2_plane = sb([P, PASSES, H], U8, "w2_plane")
+        w4_plane = sb([P, 1, N], U8, "w4_plane")
+        nc.vector.memset(w2_plane[:].bitcast(I32), 0)
+        nc.vector.memset(w4_plane[:].bitcast(I32), 0)
+        nc.vector.memset(tab_rows[32:64, :].bitcast(I32), 0)
+        nc.vector.memset(tab_rows[64:128, :].bitcast(I32), 0)
+        nc.vector.memset(v_scales[:].bitcast(I32), 0)
+
+        identity = sb([P, P], F32, "identity")
+        make_identity(nc, identity[:])
+
+        idx = lists.tile([P, S // LIST_COLS], U16, name="idx")
+        idx2 = lists.tile([P, S // LIST_COLS], U16, name="idx2")
+        idx3 = lists.tile([P, PICK // LIST_COLS], U16, name="idx3")
+        nc.sync.dma_start(idx[:], offs)
+        nc.sync.dma_start(
+            out=tab_rows[0:32, :].bitcast(I32), in_=tab_scales.rearrange("a q t -> (a q) t").bitcast(I32)
+        )
+        table = [sb([P, T], I32, "table%d" % a) for a in range(PASSES)]
+        for a in range(PASSES):
+            words = tab_words[a].rearrange("p t i -> p (t i)").bitcast(I32)
+            for half in (slice(0, T // 2), slice(T // 2, T)):
+                nc.sync.dma_start(out=table[a][:, half], in_=words[:, half])
+        w2_codes = sb([P, PASSES, 2 * H], U8, "w2_codes")
+        nc.sync.dma_start(out=w2_codes[:].bitcast(I32), in_=w2_words.rearrange("a p c -> p a c").bitcast(I32))
+        load_scale_rows(w2_plane, w2_scales)
+        picked_rows = sb([P, S], U8, "picked_rows")
+        nc.vector.tensor_copy(out=picked_rows[:], in_=tab_rows[:].indirect(idx[:]))
+        for a in range(PASSES):
+            for q in range(QUADS):
+                first = 16 * a + 4 * q
+                nc.gpsimd.dma_start(
+                    out=v_scales[QUAD * q : QUAD * q + 4, a, :].bitcast(I32),
+                    in_=picked_rows[first : first + 4, :].bitcast(I32),
+                )
+        w1_raw = [load_rows(w1[a * K_PASS : (a + 1) * K_PASS, :], "w1_raw%d" % a, "w1_raw%d" % a) for a in range(PASSES)]
+        w3_raw = [load_rows(w3[a * K_PASS : (a + 1) * K_PASS, :], "w3_raw%d" % a, "w3_raw%d" % a) for a in range(PASSES)]
+        nc.sync.dma_start(idx2[:], offs2)
+        factor = [sb([P, S], F32, "factor%d" % t) for t in range(PACK)]
+        wgs_dealt = wgs.rearrange("(q t) j -> t q j", t=PACK)
+        quad_order = (0, 2, 1, 3)
+
+        def load_factor(t):
+            for q in quad_order:
+                nc.sync.dma_start(out=factor[t][QUAD * q : QUAD * (q + 1), :], in_=wgs_dealt[t])
+
+        load_factor(0)
+        page_rows = page0.rearrange("(p t) c -> t p c", t=PACK)
+        page = [sb([P, T2], F32, "page%d" % t) for t in range(PACK)]
+        nc.sync.dma_start(out=page[0][:], in_=page_rows[0])
+        w5_raw = load_rows(w5, "w5_raw", "w1_raw0")
+        load_factor(1)
+        nc.sync.dma_start(out=page[1][:], in_=page_rows[1])
+        nc.sync.dma_start(idx3[:], offs3)
+        bias_dealt = sb([P, PACK], F32, "bias_dealt")
+        nc.sync.dma_start(out=bias_dealt[:], in_=bias.rearrange("(p t) -> p t", t=PACK))
+        w4_codes = sb([P, 2 * N], U8, "w4_codes")
+        nc.sync.dma_start(out=w4_codes[:].bitcast(I32), in_=w4_words[0].bitcast(I32))
+        load_scale_rows(w4_plane, w4_scales)
+        load_factor(2)
+        nc.sync.dma_start(out=page[2][:], in_=page_rows[2])
+        load_factor(3)
+        nc.sync.dma_start(out=page[3][:], in_=page_rows[3])
+        flav_sb = sb([P, N // P, PICK], F32, "flav_sb", "w1_raw1")
+        nc.sync.dma_start(out=flav_sb[:], in_=flav.rearrange("(n p) j -> p n j", p=P))
+
+
+        v_codes = []
+        for a in range(PASSES):
+            picked = sb([P, S], U32, "v_codes%d" % a)
+            nc.vector.tensor_copy(out=picked[:], in_=table[a][:].bitcast(U32).indirect(idx[:]))
+            v_codes.append(picked)
+
+        def first_product(j, name, w_codes, w_scales):
+            acc = bank(j, name)
+            cols = slice(j * P, (j + 1) * P)
+            for a in range(PASSES):
+                nc.tensor.matmul_mx(
+                    out=acc[:], lhsT=v_codes[a][:, cols].bitcast(FP8X4), lhsT_scale=v_scales[:, a, cols],
+                    rhs=w_codes[a], rhs_scale=w_scales[a], start=(a == 0), stop=(a == PASSES - 1),
+                )
+            return acc
+
+        upper = [sb([P, 2, PACK, P], F32, "upper%d" % c) for c in range(J_TILES // 2)]
+        lower = [sb([P, 2, PACK, P], F32, "lower%d" % c) for c in range(J_TILES // 2)]
+
+        def entry(tiles, j):
+            return tiles[j // 2][:, j % 2]
+
+        w2_c = [w2_codes[:, a, :].bitcast(FP4X4) for a in range(PASSES)]
+        w2_s = [w2_plane[:, a, :] for a in range(PASSES)]
+        for j in range(J_TILES):
+            acc = first_product(j, "b%d" % j, w2_c, w2_s)
+            nc.scalar.copy(out=entry(upper, j), in_=dealt(acc))
+
+        w1_q = [
+            quantize(weave(nc.vector.tensor_copy, w1_raw[a], "w1_woven%d" % a, "woven%d" % a), "w1_%d" % a)
+            for a in range(PASSES)
+        ]
+        w3_woven = [weave(nc.scalar.copy, w3_raw[a], "w3_woven%d" % a, ("w2_codes", "w2_plane")[a]) for a in range(PASSES)]
+        w1_c = [q[0][:].bitcast(FP8X4) for q in w1_q]
+        w1_s = [q[1][:] for q in w1_q]
+        for j in range(J_TILES):
+            acc = first_product(j, "a%d" % j, w1_c, w1_s)
+            nc.vector.tensor_tensor(out=entry(upper, j), in0=dealt(acc), in1=entry(upper, j), op=ALU.max)
+            nc.scalar.copy(out=entry(lower, j), in_=dealt(acc))
+
+        w3_q = [quantize(w3_woven[a], "w3_%d" % a) for a in range(PASSES)]
+        w3_c = [q[0][:].bitcast(FP8X4) for q in w3_q]
+        w3_s = [q[1][:] for q in w3_q]
+        for j in range(J_TILES):
+            acc = first_product(j, "e%d" % j, w3_c, w3_s)
+            nc.vector.tensor_tensor(out=entry(lower, j), in0=dealt(acc), in1=entry(lower, j), op=ALU.min)
+
+        h = sb([P, PACK, S], F32, "h", "table0")
+        for t in range(PACK):
+            for half in range(S // BANK):
+                acc = bank(2 * t + half, "h%d_%d" % (t, half))
+                for jj in range(BANK // P):
+                    j = half * (BANK // P) + jj
+                    cols = slice(jj * P, (jj + 1) * P)
+                    nc.tensor.matmul(acc[:, cols], entry(upper, j)[:, t, :], identity[:], start=True, stop=False, is_transpose=True)
+                    nc.tensor.matmul(acc[:, cols], entry(lower, j)[:, t, :], identity[:], start=False, stop=True, is_transpose=True)
+                nc.scalar.copy(out=h[:, t, half * BANK : (half + 1) * BANK], in_=acc[:])
+
+        w5_woven = weave(nc.scalar.copy, w5_raw, "w5_woven", "lower0")
+        page_woven = [sb([P, BANK, PACK], BF16, "page_woven%d" % c, "upper%d" % c) for c in range(CHUNKS)]
+        x_woven = sb([P, PICK, PACK], BF16, "x_woven", "lower1")
+        out1_rows = out_1.rearrange("(p t) c -> t p c", t=PACK)
+
+        def put(t, first, last):
+            nc.vector.tensor_tensor(
+                out=page[t][:].indirect(idx2[:, first // LIST_COLS : last // LIST_COLS]),
+                in0=h[:, t, first:last], in1=factor[t][:, first:last], op=ALU.mult,
+            )
+
+        def fetch(t):
+            cells = sb([P, PICK], F32, "cells%d" % t)
+            nc.vector.tensor_copy(out=cells[:], in_=page[t][:].indirect(idx3[:]))
+            if t < 2:
+                nc.scalar.activation(out=x_woven[:, :, t], in_=cells[:], func=ACT.Identity, bias=bias_dealt[:, t : t + 1])
+            else:
+                nc.vector.tensor_scalar(
+                    out=x_woven[:, :, t], in0=cells[:], scalar1=bias_dealt[:, t : t + 1], scalar2=None, op0=ALU.add
+                )
+
+        def hand_out(t):
+            nc.sync.dma_start(out=out1_rows[t], in_=page[t][:])
+            for c in range(CHUNKS):
+                nc.scalar.copy(out=page_woven[c][:, :, t], in_=page[t][:, c * BANK : (c + 1) * BANK])
+
+        put(0, 0, BANK)
+        put(0, BANK, S)
+        for t in range(PACK):
+            if t > 0:
+                put(t, 0, S)
+            if t == 1:
+                w5_codes, w5_scales = quantize(w5_woven, "w5", "factor1")
+            fetch(t)
+            hand_out(t)
+
+        x_codes, x_scales = quantize(x_woven, "x")
+        plane_codes = sb([P, T2], U32, "plane_codes")
+        plane_scales = sb([P, T2], U8, "plane_scales")
+        out2_words = out_2[0].rearrange("p m t -> p (m t)").bitcast(I32)
+
+        def planes(c):
+            cols = slice(c * BANK, (c + 1) * BANK)
+            nc.vector.quantize_mx(
+                out=plane_codes[:, cols].bitcast(FP8X4), scales=plane_scales[:, cols],
+                in_=page_woven[c][:].rearrange("p m t -> p (m t)"),
+            )
+            nc.sync.dma_start(out=out2_words[:, cols], in_=plane_codes[:, cols].bitcast(I32))
+
+        y = sb([P, N // P, PICK], F32, "y", "table1")
+
+        def scores(n):
+            cols = slice(n * P, (n + 1) * P)
+            m1 = bank(2 * n, "m1_%d" % n)
+            m2 = bank(2 * n + 1, "m2_%d" % n)
+            nc.tensor.matmul_mx(
+                out=m1[:], lhsT=w4_codes[:, 2 * n * P : 2 * (n + 1) * P].bitcast(FP4X4), lhsT_scale=w4_plane[:, 0, cols],
+                rhs=x_codes[:].bitcast(FP8X4), rhs_scale=x_scales[:], start=True, stop=True,
+            )
+            nc.tensor.matmul_mx(
+                out=m2[:], lhsT=w5_codes[:, cols].bitcast(FP8X4), lhsT_scale=w5_scales[:, cols],
+                rhs=x_codes[:].bitcast(FP8X4), rhs_scale=x_scales[:], start=True, stop=True,
+            )
+            nc.vector.tensor_tensor(out=y[:, n, :], in0=m1[:], in1=flav_sb[:, n, :], op=ALU.mult)
+            nc.vector.tensor_tensor(out=y[:, n, :], in0=m2[:], in1=y[:, n, :], op=ALU.add)
+            nc.sync.dma_start(out=out_0[cols, :], in_=y[:, n, :])
+
+        planes(0)
+        planes(1)
+        scores(0)
+        planes(2)
+        scores(1)
+        planes(3)
+        for q in range(QUADS):
+            nc.sync.dma_start(
+                out=out_3[0, 4 * q : 4 * q + 4, :].bitcast(I32),
+                in_=plane_scales[QUAD * q : QUAD * q + 4, :].bitcast(I32),
+            )
+        scores(2)
+        scores(3)

@@ -53,9 +53,9 @@ def tile_list_freezer_texture_page_kernel(
             nc.sync.dma_start(out=raw[:], in_=w_rows.rearrange("(p i) c -> p i c", i=PACK))
             return raw
 
-        def load_scale_rows(plane, scales):
+        def load_scale_rows(queue, plane, scales):
             for q in range(QUADS):
-                nc.sync.dma_start(
+                queue.dma_start(
                     out=plane[QUAD * q : QUAD * q + 4, :, :].bitcast(I32),
                     in_=scales[:, 4 * q : 4 * q + 4, :].rearrange("a r c -> r a c").bitcast(I32),
                 )
@@ -94,23 +94,23 @@ def tile_list_freezer_texture_page_kernel(
         idx2 = lists.tile([P, S // LIST_COLS], U16, name="idx2")
         idx3 = lists.tile([P, PICK // LIST_COLS], U16, name="idx3")
         nc.sync.dma_start(idx[:], offs)
+        w2_codes = sb([P, PASSES, 2 * H], U8, "w2_codes")
+        nc.scalar.dma_start(out=w2_codes[:].bitcast(I32), in_=w2_words.rearrange("a p c -> p a c").bitcast(I32))
+        load_scale_rows(nc.scalar, w2_plane, w2_scales)
+        table = [sb([P, T], I32, "table%d" % a) for a in range(PASSES)]
+        table_words = [tab_words[a].rearrange("p t i -> p (t i)").bitcast(I32) for a in range(PASSES)]
+        nc.sync.dma_start(out=table[0][:, : T // 4], in_=table_words[0][:, : T // 4])
         nc.sync.dma_start(
             out=tab_rows[0:32, :].bitcast(I32), in_=tab_scales.rearrange("a q t -> (a q) t").bitcast(I32)
         )
-        table = [sb([P, T], I32, "table%d" % a) for a in range(PASSES)]
-        for a in range(PASSES):
-            words = tab_words[a].rearrange("p t i -> p (t i)").bitcast(I32)
-            for half in (slice(0, T // 2), slice(T // 2, T)):
-                nc.sync.dma_start(out=table[a][:, half], in_=words[:, half])
-        w2_codes = sb([P, PASSES, 2 * H], U8, "w2_codes")
-        nc.sync.dma_start(out=w2_codes[:].bitcast(I32), in_=w2_words.rearrange("a p c -> p a c").bitcast(I32))
-        load_scale_rows(w2_plane, w2_scales)
+        nc.sync.dma_start(out=table[0][:, T // 4 :], in_=table_words[0][:, T // 4 :])
+        nc.sync.dma_start(out=table[1][:], in_=table_words[1])
         picked_rows = sb([P, S], U8, "picked_rows")
         nc.vector.tensor_copy(out=picked_rows[:], in_=tab_rows[:].indirect(idx[:]))
         for a in range(PASSES):
             for q in range(QUADS):
                 first = 16 * a + 4 * q
-                nc.gpsimd.dma_start(
+                nc.scalar.dma_start(
                     out=v_scales[QUAD * q : QUAD * q + 4, a, :].bitcast(I32),
                     in_=picked_rows[first : first + 4, :].bitcast(I32),
                 )
@@ -137,7 +137,7 @@ def tile_list_freezer_texture_page_kernel(
         nc.sync.dma_start(out=bias_dealt[:], in_=bias.rearrange("(p t) -> p t", t=PACK))
         w4_codes = sb([P, 2 * N], U8, "w4_codes")
         nc.sync.dma_start(out=w4_codes[:].bitcast(I32), in_=w4_words[0].bitcast(I32))
-        load_scale_rows(w4_plane, w4_scales)
+        load_scale_rows(nc.sync, w4_plane, w4_scales)
         load_factor(2)
         nc.sync.dma_start(out=page[2][:], in_=page_rows[2])
         load_factor(3)
@@ -152,13 +152,13 @@ def tile_list_freezer_texture_page_kernel(
             nc.vector.tensor_copy(out=picked[:], in_=table[a][:].bitcast(U32).indirect(idx[:]))
             v_codes.append(picked)
 
-        def first_product(j, name, w_codes, w_scales):
+        def first_product(j, name, w_codes, w_scales, order):
             acc = bank(j, name)
             cols = slice(j * P, (j + 1) * P)
-            for a in range(PASSES):
+            for a in order:
                 nc.tensor.matmul_mx(
                     out=acc[:], lhsT=v_codes[a][:, cols].bitcast(FP8X4), lhsT_scale=v_scales[:, a, cols],
-                    rhs=w_codes[a], rhs_scale=w_scales[a], start=(a == 0), stop=(a == PASSES - 1),
+                    rhs=w_codes[a], rhs_scale=w_scales[a], start=(a == order[0]), stop=(a == order[-1]),
                 )
             return acc
 
@@ -171,18 +171,18 @@ def tile_list_freezer_texture_page_kernel(
         w2_c = [w2_codes[:, a, :].bitcast(FP4X4) for a in range(PASSES)]
         w2_s = [w2_plane[:, a, :] for a in range(PASSES)]
         for j in range(J_TILES):
-            acc = first_product(j, "b%d" % j, w2_c, w2_s)
+            acc = first_product(j, "b%d" % j, w2_c, w2_s, (0, 1))
             nc.scalar.copy(out=entry(upper, j), in_=dealt(acc))
 
         w1_q = [
-            quantize(weave(nc.vector.tensor_copy, w1_raw[a], "w1_woven%d" % a, "woven%d" % a), "w1_%d" % a)
+            quantize(weave(nc.vector.tensor_copy, w1_raw[a], "w1_woven%d" % a, ("table1", "woven1")[a]), "w1_%d" % a)
             for a in range(PASSES)
         ]
         w3_woven = [weave(nc.scalar.copy, w3_raw[a], "w3_woven%d" % a, ("w2_codes", "w2_plane")[a]) for a in range(PASSES)]
         w1_c = [q[0][:].bitcast(FP8X4) for q in w1_q]
         w1_s = [q[1][:] for q in w1_q]
         for j in range(J_TILES):
-            acc = first_product(j, "a%d" % j, w1_c, w1_s)
+            acc = first_product(j, "a%d" % j, w1_c, w1_s, (1, 0))
             nc.vector.tensor_tensor(out=entry(upper, j), in0=dealt(acc), in1=entry(upper, j), op=ALU.max)
             nc.scalar.copy(out=entry(lower, j), in_=dealt(acc))
 
@@ -190,7 +190,7 @@ def tile_list_freezer_texture_page_kernel(
         w3_c = [q[0][:].bitcast(FP8X4) for q in w3_q]
         w3_s = [q[1][:] for q in w3_q]
         for j in range(J_TILES):
-            acc = first_product(j, "e%d" % j, w3_c, w3_s)
+            acc = first_product(j, "e%d" % j, w3_c, w3_s, (1, 0))
             nc.vector.tensor_tensor(out=entry(lower, j), in0=dealt(acc), in1=entry(lower, j), op=ALU.min)
 
         h = sb([P, PACK, S], F32, "h", "table0")
@@ -255,32 +255,38 @@ def tile_list_freezer_texture_page_kernel(
 
         y = sb([P, N // P, PICK], F32, "y", "table1")
 
-        def scores(n):
-            cols = slice(n * P, (n + 1) * P)
-            m1 = bank(2 * n, "m1_%d" % n)
-            m2 = bank(2 * n + 1, "m2_%d" % n)
+        def product(index, name, codes, scales):
+            acc = bank(index, name)
             nc.tensor.matmul_mx(
-                out=m1[:], lhsT=w4_codes[:, 2 * n * P : 2 * (n + 1) * P].bitcast(FP4X4), lhsT_scale=w4_plane[:, 0, cols],
+                out=acc[:], lhsT=codes, lhsT_scale=scales,
                 rhs=x_codes[:].bitcast(FP8X4), rhs_scale=x_scales[:], start=True, stop=True,
             )
-            nc.tensor.matmul_mx(
-                out=m2[:], lhsT=w5_codes[:, cols].bitcast(FP8X4), lhsT_scale=w5_scales[:, cols],
-                rhs=x_codes[:].bitcast(FP8X4), rhs_scale=x_scales[:], start=True, stop=True,
-            )
+            return acc
+
+        def flavoured(n):
+            m1 = product(n, "m1_%d" % n, w4_codes[:, 2 * n * P : 2 * (n + 1) * P].bitcast(FP4X4), w4_plane[:, 0, n * P : (n + 1) * P])
             nc.vector.tensor_tensor(out=y[:, n, :], in0=m1[:], in1=flav_sb[:, n, :], op=ALU.mult)
+
+        def summed(n):
+            cols = slice(n * P, (n + 1) * P)
+            m2 = product(4 + n, "m2_%d" % n, w5_codes[:, cols].bitcast(FP8X4), w5_scales[:, cols])
             nc.vector.tensor_tensor(out=y[:, n, :], in0=m2[:], in1=y[:, n, :], op=ALU.add)
             nc.sync.dma_start(out=out_0[cols, :], in_=y[:, n, :])
 
         planes(0)
         planes(1)
-        scores(0)
+        flavoured(0)
+        flavoured(1)
+        summed(0)
         planes(2)
-        scores(1)
+        flavoured(2)
+        summed(1)
+        flavoured(3)
         planes(3)
         for q in range(QUADS):
             nc.sync.dma_start(
                 out=out_3[0, 4 * q : 4 * q + 4, :].bitcast(I32),
                 in_=plane_scales[QUAD * q : QUAD * q + 4, :].bitcast(I32),
             )
-        scores(2)
-        scores(3)
+        summed(2)
+        summed(3)

@@ -78,14 +78,15 @@ def tile_list_freezer_texture_page_kernel(
             return codes, scales
 
         tab_rows = sb([P, T], U8, "tab_rows")
-        v_scales = sb([P, PASSES, S], U8, "v_scales")
+        v_scales = [sb([P, S], U8, "v_scales%d" % a) for a in range(PASSES)]
         w2_plane = sb([P, PASSES, H], U8, "w2_plane")
         w4_plane = sb([P, 1, N], U8, "w4_plane")
         nc.vector.memset(w2_plane[:].bitcast(I32), 0)
         nc.vector.memset(w4_plane[:].bitcast(I32), 0)
         nc.vector.memset(tab_rows[32:64, :].bitcast(I32), 0)
         nc.vector.memset(tab_rows[64:128, :].bitcast(I32), 0)
-        nc.vector.memset(v_scales[:].bitcast(I32), 0)
+        for a in range(PASSES):
+            nc.vector.memset(v_scales[a][:].bitcast(I32), 0)
 
         identity = sb([P, P], F32, "identity")
         make_identity(nc, identity[:])
@@ -111,7 +112,7 @@ def tile_list_freezer_texture_page_kernel(
             for q in range(QUADS):
                 first = 16 * a + 4 * q
                 nc.scalar.dma_start(
-                    out=v_scales[QUAD * q : QUAD * q + 4, a, :].bitcast(I32),
+                    out=v_scales[a][QUAD * q : QUAD * q + 4, :].bitcast(I32),
                     in_=picked_rows[first : first + 4, :].bitcast(I32),
                 )
         w1_raw = [load_rows(w1[a * K_PASS : (a + 1) * K_PASS, :], "w1_raw%d" % a, "w1_raw%d" % a) for a in range(PASSES)]
@@ -157,7 +158,7 @@ def tile_list_freezer_texture_page_kernel(
             cols = slice(j * P, (j + 1) * P)
             for a in order:
                 nc.tensor.matmul_mx(
-                    out=acc[:], lhsT=v_codes[a][:, cols].bitcast(FP8X4), lhsT_scale=v_scales[:, a, cols],
+                    out=acc[:], lhsT=v_codes[a][:, cols].bitcast(FP8X4), lhsT_scale=v_scales[a][:, cols],
                     rhs=w_codes[a], rhs_scale=w_scales[a], start=(a == order[0]), stop=(a == order[-1]),
                 )
             return acc
@@ -205,8 +206,8 @@ def tile_list_freezer_texture_page_kernel(
                 nc.scalar.copy(out=h[:, t, half * BANK : (half + 1) * BANK], in_=acc[:])
 
         w5_woven = weave(nc.scalar.copy, w5_raw, "w5_woven", "lower0")
-        page_woven = [sb([P, BANK, PACK], BF16, "page_woven%d" % c, "upper%d" % c) for c in range(CHUNKS)]
-        x_woven = sb([P, PICK, PACK], BF16, "x_woven", "lower1")
+        page_pairs = [sb([P, 2, BANK, 2], BF16, "page_pairs%d" % c, "upper%d" % c) for c in range(CHUNKS)]
+        x_rows16 = sb([P, PACK, PICK], BF16, "x_rows16", "lower1")
         out1_rows = out_1.rearrange("(p t) c -> t p c", t=PACK)
 
         def put(t, first, last):
@@ -218,17 +219,15 @@ def tile_list_freezer_texture_page_kernel(
         def fetch(t):
             cells = sb([P, PICK], F32, "cells%d" % t)
             nc.vector.tensor_copy(out=cells[:], in_=page[t][:].indirect(idx3[:]))
-            if t < 2:
-                nc.scalar.activation(out=x_woven[:, :, t], in_=cells[:], func=ACT.Identity, bias=bias_dealt[:, t : t + 1])
+            if t < PACK - 1:
+                nc.scalar.activation(out=x_rows16[:, t, :], in_=cells[:], func=ACT.Identity, bias=bias_dealt[:, t : t + 1])
             else:
                 nc.vector.tensor_scalar(
-                    out=x_woven[:, :, t], in0=cells[:], scalar1=bias_dealt[:, t : t + 1], scalar2=None, op0=ALU.add
+                    out=x_rows16[:, t, :], in0=cells[:], scalar1=bias_dealt[:, t : t + 1], scalar2=None, op0=ALU.add
                 )
 
-        def hand_out(t):
-            nc.sync.dma_start(out=out1_rows[t], in_=page[t][:])
-            for c in range(CHUNKS):
-                nc.scalar.copy(out=page_woven[c][:, :, t], in_=page[t][:, c * BANK : (c + 1) * BANK])
+        def round_page(t, c):
+            nc.scalar.copy(out=page_pairs[c][:, t // 2, :, t % 2], in_=page[t][:, c * BANK : (c + 1) * BANK])
 
         put(0, 0, BANK)
         put(0, BANK, S)
@@ -238,18 +237,27 @@ def tile_list_freezer_texture_page_kernel(
             if t == 1:
                 w5_codes, w5_scales = quantize(w5_woven, "w5", "factor1")
             fetch(t)
-            hand_out(t)
+            nc.sync.dma_start(out=out1_rows[t], in_=page[t][:])
+            if t < PACK - 1:
+                for c in range(CHUNKS):
+                    round_page(t, c)
 
-        x_codes, x_scales = quantize(x_woven, "x")
+        x_codes, x_scales = quantize(weave(nc.vector.tensor_copy, x_rows16, "x_woven", "lower2"), "x")
         plane_codes = sb([P, T2], U32, "plane_codes")
         plane_scales = sb([P, T2], U8, "plane_scales")
         out2_words = out_2[0].rearrange("p m t -> p (m t)").bitcast(I32)
 
         def planes(c):
+            round_page(PACK - 1, c)
+            woven = sb([P, BANK, PACK], BF16, "page_woven%d" % c)
+            nc.scalar.copy(
+                out=woven[:].bitcast(F32).rearrange("p (g u) w -> p g w u", u=4),
+                in_=page_pairs[c][:].rearrange("p w m e -> p w (m e)").bitcast(F32).rearrange("p w (g u) -> p g w u", u=4),
+            )
             cols = slice(c * BANK, (c + 1) * BANK)
             nc.vector.quantize_mx(
                 out=plane_codes[:, cols].bitcast(FP8X4), scales=plane_scales[:, cols],
-                in_=page_woven[c][:].rearrange("p m t -> p (m t)"),
+                in_=woven[:].rearrange("p m t -> p (m t)"),
             )
             nc.sync.dma_start(out=out2_words[:, cols], in_=plane_codes[:, cols].bitcast(I32))
 

@@ -95,15 +95,15 @@ def tile_list_freezer_texture_page_kernel(
         idx2 = lists.tile([P, S // LIST_COLS], U16, name="idx2")
         idx3 = lists.tile([P, PICK // LIST_COLS], U16, name="idx3")
         nc.sync.dma_start(idx[:], offs)
-        w2_codes = sb([P, PASSES, 2 * H], U8, "w2_codes")
-        nc.scalar.dma_start(out=w2_codes[:].bitcast(I32), in_=w2_words.rearrange("a p c -> p a c").bitcast(I32))
-        load_scale_rows(nc.scalar, w2_plane, w2_scales)
         table = [sb([P, T], I32, "table%d" % a) for a in range(PASSES)]
         table_words = [tab_words[a].rearrange("p t i -> p (t i)").bitcast(I32) for a in range(PASSES)]
         nc.sync.dma_start(out=table[0][:, : T // 4], in_=table_words[0][:, : T // 4])
         nc.sync.dma_start(
             out=tab_rows[0:32, :].bitcast(I32), in_=tab_scales.rearrange("a q t -> (a q) t").bitcast(I32)
         )
+        w2_codes = sb([P, PASSES, 2 * H], U8, "w2_codes")
+        nc.sync.dma_start(out=w2_codes[:].bitcast(I32), in_=w2_words.rearrange("a p c -> p a c").bitcast(I32))
+        load_scale_rows(nc.sync, w2_plane, w2_scales)
         nc.sync.dma_start(out=table[0][:, T // 4 :], in_=table_words[0][:, T // 4 :])
         nc.sync.dma_start(out=table[1][:], in_=table_words[1])
         picked_rows = sb([P, S], U8, "picked_rows")
@@ -111,7 +111,7 @@ def tile_list_freezer_texture_page_kernel(
         for a in range(PASSES):
             for q in range(QUADS):
                 first = 16 * a + 4 * q
-                nc.scalar.dma_start(
+                (nc.scalar, nc.gpsimd)[a].dma_start(
                     out=v_scales[a][QUAD * q : QUAD * q + 4, :].bitcast(I32),
                     in_=picked_rows[first : first + 4, :].bitcast(I32),
                 )
@@ -143,8 +143,9 @@ def tile_list_freezer_texture_page_kernel(
         nc.sync.dma_start(out=page[2][:], in_=page_rows[2])
         load_factor(3)
         nc.sync.dma_start(out=page[3][:], in_=page_rows[3])
-        flav_sb = sb([P, N // P, PICK], F32, "flav_sb", "w1_raw1")
-        nc.sync.dma_start(out=flav_sb[:], in_=flav.rearrange("(n p) j -> p n j", p=P))
+        flav_rows = [sb([P, PICK], F32, "flav%d" % n) for n in range(N // P)]
+        for n in range(N // P):
+            nc.sync.dma_start(out=flav_rows[n][:], in_=flav[n * P : (n + 1) * P, :])
 
 
         v_codes = []
@@ -179,7 +180,12 @@ def tile_list_freezer_texture_page_kernel(
             quantize(weave(nc.vector.tensor_copy, w1_raw[a], "w1_woven%d" % a, ("table1", "woven1")[a]), "w1_%d" % a)
             for a in range(PASSES)
         ]
-        w3_woven = [weave(nc.scalar.copy, w3_raw[a], "w3_woven%d" % a, ("w2_codes", "w2_plane")[a]) for a in range(PASSES)]
+        w3_woven = [sb([P, H, PACK], BF16, "w3_woven0", "woven1")]
+        nc.gpsimd.tensor_scalar(
+            out=w3_woven[0][:], in0=w3_raw[0][:].rearrange("p i c -> p c i"), scalar1=1.0, scalar2=0.0,
+            op0=ALU.mult, op1=ALU.add,
+        )
+        w3_woven.append(weave(nc.scalar.copy, w3_raw[1], "w3_woven1", "w2_plane"))
         w1_c = [q[0][:].bitcast(FP8X4) for q in w1_q]
         w1_s = [q[1][:] for q in w1_q]
         for j in range(J_TILES):
@@ -207,7 +213,8 @@ def tile_list_freezer_texture_page_kernel(
 
         w5_woven = weave(nc.scalar.copy, w5_raw, "w5_woven", "lower0")
         page_pairs = [sb([P, 2, BANK, 2], BF16, "page_pairs%d" % c, "upper%d" % c) for c in range(CHUNKS)]
-        x_rows16 = sb([P, PACK, PICK], BF16, "x_rows16", "lower1")
+        halves = [slice(0, PICK // 2), slice(PICK // 2, PICK)]
+        x_pairs = [sb([P, 2, PICK // 2, 2], BF16, "x_pairs%d" % i, "lower%d" % (1 + i)) for i in range(2)]
         out1_rows = out_1.rearrange("(p t) c -> t p c", t=PACK)
 
         def put(t, first, last):
@@ -216,15 +223,16 @@ def tile_list_freezer_texture_page_kernel(
                 in0=h[:, t, first:last], in1=factor[t][:, first:last], op=ALU.mult,
             )
 
-        def fetch(t):
-            cells = sb([P, PICK], F32, "cells%d" % t)
-            nc.vector.tensor_copy(out=cells[:], in_=page[t][:].indirect(idx3[:]))
-            if t < PACK - 1:
-                nc.scalar.activation(out=x_rows16[:, t, :], in_=cells[:], func=ACT.Identity, bias=bias_dealt[:, t : t + 1])
-            else:
-                nc.vector.tensor_scalar(
-                    out=x_rows16[:, t, :], in0=cells[:], scalar1=bias_dealt[:, t : t + 1], scalar2=None, op0=ALU.add
-                )
+        def fetch(cells, t, cols):
+            nc.vector.tensor_copy(
+                out=cells[:, cols], in_=page[t][:].indirect(idx3[:, cols.start // LIST_COLS : cols.stop // LIST_COLS])
+            )
+
+        def round_x(cells, t, i):
+            nc.scalar.activation(
+                out=x_pairs[i][:, t // 2, :, t % 2], in_=cells[:, halves[i]], func=ACT.Identity,
+                bias=bias_dealt[:, t : t + 1],
+            )
 
         def round_page(t, c):
             nc.scalar.copy(out=page_pairs[c][:, t // 2, :, t % 2], in_=page[t][:, c * BANK : (c + 1) * BANK])
@@ -236,14 +244,28 @@ def tile_list_freezer_texture_page_kernel(
                 put(t, 0, S)
             if t == 1:
                 w5_codes, w5_scales = quantize(w5_woven, "w5", "factor1")
-            fetch(t)
+            cells = sb([P, PICK], F32, "cells%d" % t)
+            for cols in halves if t == PACK - 1 else [slice(0, PICK)]:
+                fetch(cells, t, cols)
+            for i in range(2):
+                round_x(cells, t, i)
             nc.sync.dma_start(out=out1_rows[t], in_=page[t][:])
             if t < PACK - 1:
                 for c in range(CHUNKS):
                     round_page(t, c)
 
-        x_codes, x_scales = quantize(weave(nc.vector.tensor_copy, x_rows16, "x_woven", "lower2"), "x")
-        plane_codes = sb([P, T2], U32, "plane_codes")
+        x_woven = [sb([P, PICK // 2, PACK], BF16, "x_woven%d" % i) for i in range(2)]
+        x_codes = sb([P, PICK], U32, "x_codes")
+        x_scales = sb([P, PICK], U8, "x_scales")
+        for pairs, woven in zip(x_pairs, x_woven):
+            nc.vector.tensor_copy(
+                out=woven[:].bitcast(F32).rearrange("p (g u) w -> p g w u", u=4),
+                in_=pairs[:].rearrange("p w m e -> p w (m e)").bitcast(F32).rearrange("p w (g u) -> p g w u", u=4),
+            )
+        for cols, woven in zip(halves, x_woven):
+            nc.vector.quantize_mx(
+                out=x_codes[:, cols].bitcast(FP8X4), scales=x_scales[:, cols], in_=woven[:].rearrange("p c i -> p (c i)")
+            )
         plane_scales = sb([P, T2], U8, "plane_scales")
         out2_words = out_2[0].rearrange("p m t -> p (m t)").bitcast(I32)
 
@@ -255,11 +277,12 @@ def tile_list_freezer_texture_page_kernel(
                 in_=page_pairs[c][:].rearrange("p w m e -> p w (m e)").bitcast(F32).rearrange("p w (g u) -> p g w u", u=4),
             )
             cols = slice(c * BANK, (c + 1) * BANK)
+            plane_codes = sb([P, BANK], U32, "plane_codes%d" % c, "flav%d" % c if c > 0 else None)
             nc.vector.quantize_mx(
-                out=plane_codes[:, cols].bitcast(FP8X4), scales=plane_scales[:, cols],
+                out=plane_codes[:].bitcast(FP8X4), scales=plane_scales[:, cols],
                 in_=woven[:].rearrange("p m t -> p (m t)"),
             )
-            nc.sync.dma_start(out=out2_words[:, cols], in_=plane_codes[:, cols].bitcast(I32))
+            nc.sync.dma_start(out=out2_words[:, cols], in_=plane_codes[:].bitcast(I32))
 
         y = sb([P, N // P, PICK], F32, "y", "table1")
 
@@ -273,7 +296,7 @@ def tile_list_freezer_texture_page_kernel(
 
         def flavoured(n):
             m1 = product(n, "m1_%d" % n, w4_codes[:, 2 * n * P : 2 * (n + 1) * P].bitcast(FP4X4), w4_plane[:, 0, n * P : (n + 1) * P])
-            nc.vector.tensor_tensor(out=y[:, n, :], in0=m1[:], in1=flav_sb[:, n, :], op=ALU.mult)
+            nc.vector.tensor_tensor(out=y[:, n, :], in0=m1[:], in1=flav_rows[n][:], op=ALU.mult)
 
         def summed(n):
             cols = slice(n * P, (n + 1) * P)
@@ -282,19 +305,19 @@ def tile_list_freezer_texture_page_kernel(
             nc.sync.dma_start(out=out_0[cols, :], in_=y[:, n, :])
 
         planes(0)
-        planes(1)
         flavoured(0)
         flavoured(1)
         summed(0)
-        planes(2)
+        planes(1)
         flavoured(2)
         summed(1)
+        planes(2)
         flavoured(3)
+        summed(2)
+        summed(3)
         planes(3)
         for q in range(QUADS):
             nc.sync.dma_start(
                 out=out_3[0, 4 * q : 4 * q + 4, :].bitcast(I32),
                 in_=plane_scales[QUAD * q : QUAD * q + 4, :].bitcast(I32),
             )
-        summed(2)
-        summed(3)

from contextlib import ExitStack

import concourse.mybir as mybir
from concourse.masks import make_identity

K, T, S, H, T2, PICK, N = 1024, 4096, 1024, 512, 2048, 512, 512
FLOPS = 2 * (3 * K * H * S + 2 * H * N * PICK)

F32 = mybir.dt.float32
BF16 = mybir.dt.bfloat16
I32 = mybir.dt.int32
U32 = mybir.dt.uint32
U16 = mybir.dt.uint16
U8 = mybir.dt.uint8
FP8X4 = mybir.dt.float8_e4m3fn_x4
FP4X4 = mybir.dt.float4_e2m1fn_x4
ALU = mybir.AluOpType
ACT = mybir.ActivationFunctionType

P = 128
PACK = 4
K_PASS = P * PACK
PASSES = K // K_PASS
BANK = 512
J_TILES = S // P
QUADS = 4
QUAD = 32
CHUNKS = T2 // BANK
LIST_COLS = 16


def tile_list_freezer_texture_page_kernel(
    tc, tab_words, tab_scales, offs, offs2, offs3, w1, w2_words, w2_scales, w3, wgs, page0, bias,
    w4_words, w4_scales, w5, flav, out_0, out_1, out_2, out_3,
):
    nc = tc.nc
    with ExitStack() as ctx:
        lists = ctx.enter_context(tc.tile_pool(name="lists", bufs=1))
        keep = ctx.enter_context(tc.tile_pool(name="keep", bufs=1))
        psum = ctx.enter_context(tc.psum_pool(name="psum", bufs=1))

        def sb(shape, dtype, name, tag=None):
            return keep.tile(shape, dtype, name=name, tag=tag or name, align_bytes=64)

        def bank(index, name):
            return psum.tile([P, BANK], F32, name=name, tag="bank%d" % index)

        def dealt(bank_tile):
            return bank_tile[:].rearrange("p (m t) -> p t m", t=PACK)

        def load_rows(w_rows, name, tag):
            raw = sb([P, PACK, H], F32, name, tag)
            nc.sync.dma_start(out=raw[:], in_=w_rows.rearrange("(p i) c -> p i c", i=PACK))
            return raw

        def load_scale_rows(queue, plane, scales):
            for q in range(QUADS):
                queue.dma_start(
                    out=plane[QUAD * q : QUAD * q + 4, :, :].bitcast(I32),
                    in_=scales[:, 4 * q : 4 * q + 4, :].rearrange("a r c -> r a c").bitcast(I32),
                )

        def weave(copy, raw, name, tag):
            woven = sb([P, H, PACK], BF16, name, tag)
            copy(
                out=woven[:].rearrange("p (c u) i -> p c i u", u=4),
                in_=raw[:].rearrange("p i (c u) -> p c i u", u=4),
            )
            return woven

        def quantize(woven, name, tag=None):
            width = woven.shape[1]
            codes = sb([P, width], U32, name + "_codes", tag)
            scales = sb([P, width], U8, name + "_scales")
            nc.vector.quantize_mx(
                out=codes[:].bitcast(FP8X4), scales=scales[:], in_=woven[:].rearrange("p c i -> p (c i)")
            )
            return codes, scales

        tab_rows = sb([P, T], U8, "tab_rows")
        v_scales = [sb([P, S], U8, "v_scales%d" % a) for a in range(PASSES)]
        w2_plane = sb([P, PASSES, H], U8, "w2_plane")
        w4_plane = sb([P, 1, N], U8, "w4_plane")
        nc.vector.memset(w2_plane[:].bitcast(I32), 0)
        nc.vector.memset(w4_plane[:].bitcast(I32), 0)
        nc.vector.memset(tab_rows[32:64, :].bitcast(I32), 0)
        nc.vector.memset(tab_rows[64:128, :].bitcast(I32), 0)
        for a in range(PASSES):
            nc.vector.memset(v_scales[a][:].bitcast(I32), 0)

        identity = sb([P, P], F32, "identity")
        make_identity(nc, identity[:])

        idx = lists.tile([P, S // LIST_COLS], U16, name="idx")
        idx2 = lists.tile([P, S // LIST_COLS], U16, name="idx2")
        idx3 = lists.tile([P, PICK // LIST_COLS], U16, name="idx3")
        nc.sync.dma_start(idx[:], offs)
        table = [sb([P, T], I32, "table%d" % a) for a in range(PASSES)]
        table_words = [tab_words[a].rearrange("p t i -> p (t i)").bitcast(I32) for a in range(PASSES)]
        nc.sync.dma_start(out=table[0][:, : T // 4], in_=table_words[0][:, : T // 4])
        nc.sync.dma_start(
            out=tab_rows[0:32, :].bitcast(I32), in_=tab_scales.rearrange("a q t -> (a q) t").bitcast(I32)
        )
        w2_codes = sb([P, PASSES, 2 * H], U8, "w2_codes")
        nc.sync.dma_start(out=w2_codes[:].bitcast(I32), in_=w2_words.rearrange("a p c -> p a c").bitcast(I32))
        load_scale_rows(nc.sync, w2_plane, w2_scales)
        nc.sync.dma_start(out=table[0][:, T // 4 :], in_=table_words[0][:, T // 4 :])
        nc.sync.dma_start(out=table[1][:], in_=table_words[1])
        picked_rows = sb([P, S], U8, "picked_rows")
        nc.vector.tensor_copy(out=picked_rows[:], in_=tab_rows[:].indirect(idx[:]))
        for a in range(PASSES):
            for q in range(QUADS):
                first = 16 * a + 4 * q
                (nc.scalar, nc.gpsimd)[a].dma_start(
                    out=v_scales[a][QUAD * q : QUAD * q + 4, :].bitcast(I32),
                    in_=picked_rows[first : first + 4, :].bitcast(I32),
                )
        w1_raw = [load_rows(w1[a * K_PASS : (a + 1) * K_PASS, :], "w1_raw%d" % a, "w1_raw%d" % a) for a in range(PASSES)]
        w3_raw = [load_rows(w3[a * K_PASS : (a + 1) * K_PASS, :], "w3_raw%d" % a, "w3_raw%d" % a) for a in range(PASSES)]
        nc.sync.dma_start(idx2[:], offs2)
        factor = [sb([P, S], F32, "factor%d" % t) for t in range(PACK)]
        wgs_dealt = wgs.rearrange("(q t) j -> t q j", t=PACK)
        quad_order = (0, 2, 1, 3)

        def load_factor(t):
            for q in quad_order:
                nc.sync.dma_start(out=factor[t][QUAD * q : QUAD * (q + 1), :], in_=wgs_dealt[t])

        load_factor(0)
        page_rows = page0.rearrange("(p t) c -> t p c", t=PACK)
        page = [sb([P, T2], F32, "page%d" % t) for t in range(PACK)]
        nc.sync.dma_start(out=page[0][:], in_=page_rows[0])
        w5_raw = load_rows(w5, "w5_raw", "w1_raw0")
        load_factor(1)
        nc.sync.dma_start(out=page[1][:], in_=page_rows[1])
        nc.sync.dma_start(idx3[:], offs3)
        bias_dealt = sb([P, PACK], F32, "bias_dealt")
        nc.sync.dma_start(out=bias_dealt[:], in_=bias.rearrange("(p t) -> p t", t=PACK))
        w4_codes = sb([P, 2 * N], U8, "w4_codes")
        nc.sync.dma_start(out=w4_codes[:].bitcast(I32), in_=w4_words[0].bitcast(I32))
        load_scale_rows(nc.sync, w4_plane, w4_scales)
        load_factor(2)
        nc.sync.dma_start(out=page[2][:], in_=page_rows[2])
        load_factor(3)
        nc.sync.dma_start(out=page[3][:], in_=page_rows[3])
        flav_rows = [sb([P, PICK], F32, "flav%d" % n) for n in range(N // P)]
        for n in range(N // P):
            nc.sync.dma_start(out=flav_rows[n][:], in_=flav[n * P : (n + 1) * P, :])


        v_codes = []
        for a in range(PASSES):
            picked = sb([P, S], U32, "v_codes%d" % a)
            nc.vector.tensor_copy(out=picked[:], in_=table[a][:].bitcast(U32).indirect(idx[:]))
            v_codes.append(picked)

        def first_product(j, name, w_codes, w_scales, order):
            acc = bank(j, name)
            cols = slice(j * P, (j + 1) * P)
            for a in order:
                nc.tensor.matmul_mx(
                    out=acc[:], lhsT=v_codes[a][:, cols].bitcast(FP8X4), lhsT_scale=v_scales[a][:, cols],
                    rhs=w_codes[a], rhs_scale=w_scales[a], start=(a == order[0]), stop=(a == order[-1]),
                )
            return acc

        upper = [sb([P, 2, PACK, P], F32, "upper%d" % c) for c in range(J_TILES // 2)]
        lower = [sb([P, 2, PACK, P], F32, "lower%d" % c) for c in range(J_TILES // 2)]

        def entry(tiles, j):
            return tiles[j // 2][:, j % 2]

        w2_c = [w2_codes[:, a, :].bitcast(FP4X4) for a in range(PASSES)]
        w2_s = [w2_plane[:, a, :] for a in range(PASSES)]
        for j in range(J_TILES):
            acc = first_product(j, "b%d" % j, w2_c, w2_s, (0, 1))
            nc.scalar.copy(out=entry(upper, j), in_=dealt(acc))

        w1_q = [
            quantize(weave(nc.vector.tensor_copy, w1_raw[a], "w1_woven%d" % a, ("table1", "woven1")[a]), "w1_%d" % a)
            for a in range(PASSES)
        ]
        w3_woven = [sb([P, H, PACK], BF16, "w3_woven0", "woven1")]
        nc.gpsimd.tensor_scalar(
            out=w3_woven[0][:], in0=w3_raw[0][:].rearrange("p i c -> p c i"), scalar1=1.0, scalar2=0.0,
            op0=ALU.mult, op1=ALU.add,
        )
        w3_woven.append(weave(nc.scalar.copy, w3_raw[1], "w3_woven1", "w2_plane"))
        w1_c = [q[0][:].bitcast(FP8X4) for q in w1_q]
        w1_s = [q[1][:] for q in w1_q]
        for j in range(J_TILES):
            acc = first_product(j, "a%d" % j, w1_c, w1_s, (1, 0))
            nc.vector.tensor_tensor(out=entry(upper, j), in0=dealt(acc), in1=entry(upper, j), op=ALU.max)
            nc.scalar.copy(out=entry(lower, j), in_=dealt(acc))

        w3_q = [quantize(w3_woven[a], "w3_%d" % a) for a in range(PASSES)]
        w3_c = [q[0][:].bitcast(FP8X4) for q in w3_q]
        w3_s = [q[1][:] for q in w3_q]
        for j in range(J_TILES):
            acc = first_product(j, "e%d" % j, w3_c, w3_s, (1, 0))
            nc.vector.tensor_tensor(out=entry(lower, j), in0=dealt(acc), in1=entry(lower, j), op=ALU.min)

        h = sb([P, PACK, S], F32, "h", "table0")
        for t in range(PACK):
            for half in range(S // BANK):
                acc = bank(2 * t + half, "h%d_%d" % (t, half))
                for jj in range(BANK // P):
                    j = half * (BANK // P) + jj
                    cols = slice(jj * P, (jj + 1) * P)
                    nc.tensor.matmul(acc[:, cols], entry(upper, j)[:, t, :], identity[:], start=True, stop=False, is_transpose=True)
                    nc.tensor.matmul(acc[:, cols], entry(lower, j)[:, t, :], identity[:], start=False, stop=True, is_transpose=True)
                nc.scalar.copy(out=h[:, t, half * BANK : (half + 1) * BANK], in_=acc[:])

        w5_woven = weave(nc.scalar.copy, w5_raw, "w5_woven", "lower0")
        page_pairs = [sb([P, 2, BANK, 2], BF16, "page_pairs%d" % c, "upper%d" % c) for c in range(CHUNKS)]
        halves = [slice(0, PICK // 2), slice(PICK // 2, PICK)]
        x_pairs = [sb([P, 2, PICK // 2, 2], BF16, "x_pairs%d" % i, "lower%d" % (1 + i)) for i in range(2)]
        out1_rows = out_1.rearrange("(p t) c -> t p c", t=PACK)

        def put(t, first, last):
            nc.vector.tensor_tensor(
                out=page[t][:].indirect(idx2[:, first // LIST_COLS : last // LIST_COLS]),
                in0=h[:, t, first:last], in1=factor[t][:, first:last], op=ALU.mult,
            )

        def fetch(cells, t, cols):
            nc.vector.tensor_copy(
                out=cells[:, cols], in_=page[t][:].indirect(idx3[:, cols.start // LIST_COLS : cols.stop // LIST_COLS])
            )

        def round_x(cells, t, i):
            nc.scalar.activation(
                out=x_pairs[i][:, t // 2, :, t % 2], in_=cells[:, halves[i]], func=ACT.Identity,
                bias=bias_dealt[:, t : t + 1],
            )

        def round_page(t, c):
            nc.scalar.copy(out=page_pairs[c][:, t // 2, :, t % 2], in_=page[t][:, c * BANK : (c + 1) * BANK])

        put(0, 0, BANK)
        put(0, BANK, S)
        for t in range(PACK):
            if t > 0:
                put(t, 0, S)
            if t == 1:
                w5_codes, w5_scales = quantize(w5_woven, "w5", "factor1")
            cells = sb([P, PICK], F32, "cells%d" % t)
            for cols in halves if t == PACK - 1 else [slice(0, PICK)]:
                fetch(cells, t, cols)
            for i in range(2):
                round_x(cells, t, i)
            nc.sync.dma_start(out=out1_rows[t], in_=page[t][:])
            if t < PACK - 1:
                for c in range(CHUNKS):
                    round_page(t, c)

        x_woven = [sb([P, PICK // 2, PACK], BF16, "x_woven%d" % i) for i in range(2)]
        x_codes = sb([P, PICK], U32, "x_codes")
        x_scales = sb([P, PICK], U8, "x_scales")
        for pairs, woven in zip(x_pairs, x_woven):
            nc.vector.tensor_copy(
                out=woven[:].bitcast(F32).rearrange("p (g u) w -> p g w u", u=4),
                in_=pairs[:].rearrange("p w m e -> p w (m e)").bitcast(F32).rearrange("p w (g u) -> p g w u", u=4),
            )
        for cols, woven in zip(halves, x_woven):
            nc.vector.quantize_mx(
                out=x_codes[:, cols].bitcast(FP8X4), scales=x_scales[:, cols], in_=woven[:].rearrange("p c i -> p (c i)")
            )
        plane_scales = sb([P, T2], U8, "plane_scales")
        out2_words = out_2[0].rearrange("p m t -> p (m t)").bitcast(I32)

        def planes(c):
            round_page(PACK - 1, c)
            woven = sb([P, BANK, PACK], BF16, "page_woven%d" % c)
            nc.scalar.copy(
                out=woven[:].bitcast(F32).rearrange("p (g u) w -> p g w u", u=4),
                in_=page_pairs[c][:].rearrange("p w m e -> p w (m e)").bitcast(F32).rearrange("p w (g u) -> p g w u", u=4),
            )
            cols = slice(c * BANK, (c + 1) * BANK)
            plane_codes = sb([P, BANK], U32, "plane_codes%d" % c, "flav%d" % c if c > 0 else None)
            nc.vector.quantize_mx(
                out=plane_codes[:].bitcast(FP8X4), scales=plane_scales[:, cols],
                in_=woven[:].rearrange("p m t -> p (m t)"),
            )
            nc.sync.dma_start(out=out2_words[:, cols], in_=plane_codes[:].bitcast(I32))

        y = sb([P, N // P, PICK], F32, "y", "table1")

        def product(index, name, codes, scales):
            acc = bank(index, name)
            nc.tensor.matmul_mx(
                out=acc[:], lhsT=codes, lhsT_scale=scales,
                rhs=x_codes[:].bitcast(FP8X4), rhs_scale=x_scales[:], start=True, stop=True,
            )
            return acc

        def flavoured(n):
            m1 = product(n, "m1_%d" % n, w4_codes[:, 2 * n * P : 2 * (n + 1) * P].bitcast(FP4X4), w4_plane[:, 0, n * P : (n + 1) * P])
            nc.vector.tensor_tensor(out=y[:, n, :], in0=m1[:], in1=flav_rows[n][:], op=ALU.mult)

        def summed(n):
            cols = slice(n * P, (n + 1) * P)
            m2 = product(4 + n, "m2_%d" % n, w5_codes[:, cols].bitcast(FP8X4), w5_scales[:, cols])
            nc.vector.tensor_tensor(out=y[:, n, :], in0=m2[:], in1=y[:, n, :], op=ALU.add)
            nc.sync.dma_start(out=out_0[cols, :], in_=y[:, n, :])

        planes(0)
        flavoured(0)
        flavoured(1)
        summed(0)
        planes(1)
        flavoured(2)
        summed(1)
        planes(2)
        flavoured(3)
        summed(2)
        summed(3)
        planes(3)
        for q in range(QUADS):
            nc.sync.dma_start(
                out=out_3[0, 4 * q : 4 * q + 4, :].bitcast(I32),
                in_=plane_scales[QUAD * q : QUAD * q + 4, :].bitcast(I32),
            )
